import numpy as np
import ml_dtypes


def mxq(x, axis, fmt="e4m3"):
    dtype, down = {"e4m3": (ml_dtypes.float8_e4m3fn, 7), "e5m2": (ml_dtypes.float8_e5m2, 14)}[fmt]
    v = np.moveaxis(np.asarray(x, np.float32).astype(ml_dtypes.bfloat16).astype(np.float64), axis, -1)
    blocks = v.reshape(v.shape[:-1] + (-1, 32))
    amax = np.abs(blocks).max(-1, keepdims=True)
    byte = np.maximum(np.where(amax > 0, np.frexp(amax)[1] - 1 + 127, 0) - down, 1)
    scale = np.exp2(byte - 127.0)
    codes = (blocks / scale).astype(np.float32).astype(dtype).astype(np.float64)
    return np.moveaxis((codes * scale).reshape(v.shape), -1, axis)


WIDE = False


def mx_kscale(k):
    if not WIDE:
        return np.ones(k)
    levels = np.array([10, -10, 5, -5, 0])
    if k % 512:
        return np.exp2(np.random.permutation(np.resize(levels, k // 32))).repeat(32)
    a = np.empty((k // 512, 16))
    for p in range(k // 512):
        a[p, :8] = np.random.permutation(np.resize(levels, 8))
        for g in range(8):
            far = levels[np.abs(levels - a[p, g]) >= 10]
            a[p, g + 8] = far[np.random.randint(len(far))]
    return np.exp2(a.ravel()).repeat(32)


def f64(x):
    return np.asarray(x).astype(np.float64)


def striped(idx):
    return np.tile(idx.reshape(-1, 16).T, (8, 1)).astype(np.uint16)


def unstriped(offs):
    return offs[:16].T.reshape(-1).astype(np.int64)


E2M1 = np.array([0.0, 0.5, 1.0, 1.5, 2.0, 3.0, 4.0, 6.0, -0.0, -0.5, -1.0, -1.5, -2.0, -3.0, -4.0, -6.0])


def pack_weight(w, fmt):
    k, n = w.shape
    w = f64(np.asarray(w, np.float32).astype(ml_dtypes.bfloat16)).reshape(k // 32, 32, n)
    amax = np.abs(w).max(1)
    if fmt == "e4m3":
        byte = np.frexp(amax)[1] - 1 + 127 - 7
    else:
        mant, ex = np.frexp(amax / 6.0)
        byte = np.where(mant > 0.5, ex, ex - 1) + 127
    byte = np.clip(np.where(amax > 0, byte, 1), 1, 254)
    scaled = (w * np.exp2(127.0 - byte)[:, None, :]).reshape(k, n).astype(np.float32)
    by_word = np.ascontiguousarray(scaled.reshape(k // 512, 128, 4, n).transpose(0, 1, 3, 2))
    if fmt == "e4m3":
        words = by_word.astype(ml_dtypes.float8_e4m3fn).view(np.uint8)
    else:
        c = by_word.astype(ml_dtypes.float4_e2m1fn).view(np.uint8) & 0xF
        words = (c[..., 0::2] | (c[..., 1::2] << 4)).reshape(k // 512, 128, 2 * n)
    return np.ascontiguousarray(words), np.ascontiguousarray(byte.astype(np.uint8).reshape(k // 512, 16, n))


def unpack_weight(words, scales, fmt):
    g, _, n = scales.shape
    words = np.ascontiguousarray(words).reshape(g, 128, n, -1)
    if fmt == "e4m3":
        vals = words.view(ml_dtypes.float8_e4m3fn).astype(np.float64)
    else:
        nib = np.empty((g, 128, n, 4), np.uint8)
        nib[..., 0::2] = words & 0xF
        nib[..., 1::2] = words >> 4
        vals = E2M1[nib]
    vals = vals * np.repeat(np.exp2(scales.astype(np.float64) - 127.0), 8, axis=1)[..., None]
    return vals.transpose(0, 1, 3, 2).reshape(g * 512, n)


def gelu(v):
    return 0.5 * v * (1.0 + np.tanh(np.sqrt(2.0 / np.pi) * (v + 0.044715 * v**3)))


K, K2, H, N, T, S, P, T2 = 1024, 512, 512, 384, 2048, 1024, 512, 2048


def setup_inputs():
    n = np.random.standard_normal
    s, s2, u = mx_kscale(K)[:, None], mx_kscale(K2)[:, None], mx_kscale(H)[:, None]
    perm = np.random.permutation(T2)
    tab_words, tab_scales = pack_weight(n((K, T)) * s, "e4m3")
    tab2_words, tab2_scales = pack_weight(n((K2, T)) * s2, "e4m3")
    w2_words, w2_scales = pack_weight(1.4 * n((K, H)) / np.sqrt(K) / s, "e2m1")
    w5_words, w5_scales = pack_weight(0.7 * n((K, N)) / np.sqrt(K) / s, "e4m3")
    return {
        "tab_words": tab_words, "tab_scales": tab_scales, "tab2_words": tab2_words, "tab2_scales": tab2_scales,
        "offs": striped(np.random.permutation(T)[:S]), "offs2": striped(np.random.permutation(T)[:P]),
        "pos1": striped(np.random.permutation(S)[:P]),
        "offs3": striped(perm[:S]), "offs4": striped(perm[S:S + P]),
        "w1": (1.4 * n((K, H)) / np.sqrt(K) / s).astype(np.float32),
        "w2_words": w2_words, "w2_scales": w2_scales,
        "w3": (n((K2, H)) / np.sqrt(K2) / s2 * u.T).astype(np.float32),
        "gain": (np.exp(0.3 * n(H)) * u[:, 0]).astype(np.float32),
        "w4": (1.3 * n((H, N)) / np.sqrt(H) / u).astype(np.float32),
        "w5_words": w5_words, "w5_scales": w5_scales,
        "w6": (n((H, N)) / np.sqrt(H) / u).astype(np.float32),
        "page1": n((N, T2)).astype(np.float32),
        "wg1": np.exp(0.3 * n((128, S))).astype(np.float32), "wg2": np.exp(0.3 * n((128, P))).astype(np.float32),
    }


def reference(tab_words, tab_scales, tab2_words, tab2_scales, offs, offs2, pos1, offs3, offs4, w1, w2_words, w2_scales,
              w3, gain, w4, w5_words, w5_scales, w6, page1, wg1, wg2):
    v = unpack_weight(tab_words, tab_scales, "e4m3")[:, unstriped(offs)]
    v2 = unpack_weight(tab2_words, tab2_scales, "e4m3")[:, unstriped(offs2)]
    h1 = np.maximum(mxq(f64(w1), 0, "e4m3").T @ v, unpack_weight(w2_words, w2_scales, "e2m1").T @ v)
    h2 = mxq(f64(w3), 0, "e4m3").T @ v2
    z1 = mxq(np.tanh(h1) * f64(gain)[:, None], 0, "e4m3")
    z2 = mxq(h2 * h1[:, unstriped(pos1)], 0, "e4m3")
    y1 = mxq(f64(w4), 0, "e4m3").T @ z1 + unpack_weight(w5_words, w5_scales, "e4m3").T @ v
    y2 = mxq(f64(w6), 0, "e4m3").T @ z2
    out = f64(page1).copy()
    out[:, unstriped(offs3)] = np.tile(f64(wg1), (N // 128, 1)) * y1
    out[:, unstriped(offs4)] = np.tile(f64(wg2), (N // 128, 1)) * y2
    return out

@@ -1,0 +1,251 @@
+from contextlib import ExitStack
+
+import concourse.mybir as mybir
+
+K, K2, H, N, T, S, B, T2 = 1024, 512, 512, 384, 2048, 1024, 512, 2048
+FLOPS = 2 * (2 * K * H * S + K2 * H * B + H * N * S + K * N * S + H * N * B)
+
+F32 = mybir.dt.float32
+BF16 = mybir.dt.bfloat16
+I32 = mybir.dt.int32
+U32 = mybir.dt.uint32
+U16 = mybir.dt.uint16
+U8 = mybir.dt.uint8
+FP8X4 = mybir.dt.float8_e4m3fn_x4
+FP4X4 = mybir.dt.float4_e2m1fn_x4
+MULT = mybir.AluOpType.mult
+MAX = mybir.AluOpType.max
+COPY = mybir.ActivationFunctionType.Copy
+TANH = mybir.ActivationFunctionType.Tanh
+
+P = 128
+PACK = 4
+K_PASS = P * PACK
+PASSES = K // K_PASS
+QUADS = 4
+ROW_BLOCKS = N // P
+CHUNK = 256
+CHUNKS = S // CHUNK
+BANK = 512
+
+
+def tile_list_showroom_slot_features_kernel(
+    tc, tab_words, tab_scales, tab2_words, tab2_scales, offs, offs2, pos1, offs3, offs4, w1, w2_words, w2_scales,
+    w3, gain, w4, w5_words, w5_scales, w6, page1, wg1, wg2, out,
+):
+    nc = tc.nc
+    with ExitStack() as ctx:
+        keep = ctx.enter_context(tc.tile_pool(name="keep", bufs=1))
+        ring = ctx.enter_context(tc.tile_pool(name="ring", bufs=2))
+        psum = ctx.enter_context(tc.psum_pool(name="psum", bufs=2))
+
+        def held(name, shape, dtype):
+            return keep.tile(shape, dtype, name=name, align_bytes=64)
+
+        def load_list(name, src):
+            tile = keep.tile([P, src.shape[1]], U16, name=name)
+            nc.sync.dma_start(tile[:], src)
+            return tile
+
+        def load_planes(queue, clear, name, src):
+            passes, width = src.shape[0], src.shape[2]
+            tile = held(name, [P, passes * width], U8)
+            clear.memset(tile[:].bitcast(I32), 0)
+            for q in range(QUADS):
+                queue.dma_start(
+                    tile[32 * q : 32 * q + 4, :].bitcast(I32).rearrange("r (a c) -> r a c", a=passes),
+                    src[:, 4 * q : 4 * q + 4, :].bitcast(I32).rearrange("a r c -> r a c"),
+                )
+            return tile
+
+        def load_table_pass(name, words):
+            tile = held(name, [P, T], U32)
+            nc.sync.dma_start(tile[:].bitcast(I32), words.rearrange("p t i -> p (t i)").bitcast(I32))
+            return tile
+
+        def load_first_weight(name, rows):
+            tile = held(name, [P, PACK, H], F32)
+            nc.sync.dma_start(tile[:], rows.rearrange("(p j) c -> p j c", j=PACK))
+            return tile
+
+        def load_second_weight(name, w):
+            tile = held(name, [P, PACK, N], F32)
+            rows = w.rearrange("(u t e) n -> t u e n", t=PACK, e=4)
+            for t in range(PACK):
+                nc.sync.dma_start(tile[:, t, :], rows[t])
+            return tile
+
+        def gather(name, window, offsets, dtype):
+            tile = held(name, [P, 16 * offsets.shape[1]], dtype)
+            nc.vector.tensor_copy(tile[:], window.indirect(offsets))
+            return tile
+
+        def quantize(name, grouped, width):
+            codes = held(name + "_codes", [P, width], U32)
+            scales = held(name + "_scales", [P, width], U8)
+            nc.vector.quantize_mx(out=codes[:].bitcast(FP8X4), scales=scales[:], in_=grouped[:, 0 : PACK * width])
+            return codes, scales
+
+        def round_first_weight(move, raw):
+            grouped = ring.tile([P, PACK * H], BF16, name="weight_bf16", align_bytes=64)
+            move(
+                grouped[:].rearrange("p (t u e j) -> p t u j e", t=PACK, e=4, j=PACK),
+                raw[:].rearrange("p j (u t e) -> p t u j e", t=PACK, e=4),
+            )
+            return grouped
+
+        def interleave(move, tag, rows, width):
+            grouped = ring.tile([P, PACK * BANK], BF16, name=tag, align_bytes=64)
+            move(
+                grouped[:, 0 : PACK * width].rearrange("p (c i t) -> p c t i", i=4, t=PACK),
+                rows.rearrange("p t (c i) -> p c t i", i=4),
+            )
+            return grouped
+
+        def passes_into(acc, passes):
+            for i, (w_codes, w_scales, x_codes, x_scales) in enumerate(passes):
+                nc.tensor.matmul_mx(out=acc, lhsT=w_codes, lhsT_scale=w_scales, rhs=x_codes, rhs_scale=x_scales,
+                                    start=(i == 0), stop=(i == len(passes) - 1))
+
+        idx = load_list("idx", offs)
+        tab_planes = load_planes(nc.scalar, nc.vector, "tab_planes", tab_scales)
+        tab_sb = [None] * PASSES
+        tab_sb[0] = load_table_pass("tab0", tab_words[0])
+        w2_planes_raw = load_planes(nc.sync, nc.gpsimd, "w2_planes_raw", w2_scales)
+        w2_raw = held("w2_raw", [P, PASSES, H // 2], I32)
+        nc.sync.dma_start(w2_raw[:], w2_words.bitcast(I32).rearrange("a p c -> p a c"))
+        w1_raw = [load_first_weight("w1_raw%d" % a, w1[a * K_PASS : (a + 1) * K_PASS, :]) for a in range(PASSES)]
+        tab_sb[1] = load_table_pass("tab1", tab_words[1])
+        gains = held("gains", [P, PACK], F32)
+        with nc.allow_non_contiguous_dma(reason="one gain to a partition and slot"):
+            for e in range(4):
+                nc.sync.dma_start(gains[e:P:4, :], gain.rearrange("(u t e) -> e u t", t=PACK, e=4)[e])
+        w4_raw = load_second_weight("w4_raw", w4)
+        w5_codes = held("w5_codes", [P, PASSES, N], U32)
+        nc.sync.dma_start(w5_codes[:].bitcast(I32), w5_words.rearrange("a p c i -> p a (c i)").bitcast(I32))
+        w5_planes = load_planes(nc.sync, nc.gpsimd, "w5_planes", w5_scales)
+        idx3 = load_list("idx3", offs3)
+        wg1_sb = held("wg1_sb", [P, S], F32)
+        nc.sync.dma_start(wg1_sb[:], wg1)
+        pages = []
+        for b in range(ROW_BLOCKS):
+            page = held("page%d" % b, [P, T2], F32)
+            nc.sync.dma_start(page[:], page1[b * P : (b + 1) * P, :])
+            pages.append(page)
+        idx2 = load_list("idx2", offs2)
+        tab2_sb = load_table_pass("tab2", tab2_words[0])
+        tab2_plane = load_planes(nc.sync, nc.gpsimd, "tab2_plane", tab2_scales)
+        w3_raw = load_first_weight("w3_raw", w3)
+        hero = load_list("hero", pos1)
+        w6_raw = load_second_weight("w6_raw", w6)
+        idx4 = load_list("idx4", offs4)
+        wg2_sb = held("wg2_sb", [P, B], F32)
+        nc.sync.dma_start(wg2_sb[:], wg2)
+
+        v_words0 = gather("v_words0", tab_sb[0][:], idx[:], U32)
+        first_cols = CHUNK // 16
+        planes_first = [gather("v_plane_first%d" % a, tab_planes[:, a * T : (a + 1) * T], idx[:, 0:first_cols], U8)
+                        for a in range(PASSES)]
+        w2_codes = held("w2_codes", [P, PASSES * 2 * H], U8)
+        nc.vector.tensor_copy(
+            w2_codes[:].bitcast(I32).rearrange("p (a t u h) -> p a t u h", a=PASSES, t=PACK, h=2),
+            w2_raw[:].rearrange("p a (u t h) -> p a t u h", t=PACK, h=2),
+        )
+        w2_planes = held("w2_planes", [P, PASSES * H], U8)
+        nc.vector.tensor_copy(
+            w2_planes[:].bitcast(I32).rearrange("p (a t u) -> p a t u", a=PASSES, t=PACK),
+            w2_planes_raw[:].bitcast(I32).rearrange("p (a u t) -> p a t u", a=PASSES, t=PACK),
+        )
+        w1_q = [quantize("w1_%d" % a, round_first_weight(nc.scalar.copy, w1_raw[a]), H) for a in range(PASSES)]
+        v_words1_first = gather("v_words1_first", tab_sb[1][:], idx[:, 0:first_cols], U32)
+        v_words1_rest = gather("v_words1_rest", tab_sb[1][:], idx[:, first_cols : S // 16], U32)
+        planes_rest = [gather("v_plane_rest%d" % a, tab_planes[:, a * T : (a + 1) * T], idx[:, first_cols : S // 16], U8)
+                       for a in range(PASSES)]
+
+        def v_operand(a, c):
+            cols = slice(c * CHUNK, (c + 1) * CHUNK)
+            if a == 0:
+                words = v_words0[:, cols]
+            elif c == 0:
+                words = v_words1_first[:]
+            else:
+                words = v_words1_rest[:, (c - 1) * CHUNK : c * CHUNK]
+            plane = planes_first[a][:] if c == 0 else planes_rest[a][:, (c - 1) * CHUNK : c * CHUNK]
+            return words.bitcast(FP8X4), plane
+
+        h1 = [held("h1_%d" % t, [P, S], F32) for t in range(PACK)]
+
+        def first_stage(c):
+            cols = slice(c * CHUNK, (c + 1) * CHUNK)
+            for t in range(PACK):
+                m = slice(t * P, (t + 1) * P)
+                acc = psum.tile([P, 2, CHUNK], F32, name="acc_h1", bufs=4)
+                passes_into(acc[:, 1, 0:CHUNK], [
+                    (w2_codes[:, 2 * (a * H + t * P) : 2 * (a * H + (t + 1) * P)].bitcast(FP4X4),
+                     w2_planes[:, a * H + t * P : a * H + (t + 1) * P]) + v_operand(a, c) for a in range(PASSES)])
+                passes_into(acc[:, 0, 0:CHUNK], [
+                    (w1_q[a][0][:, m].bitcast(FP8X4), w1_q[a][1][:, m]) + v_operand(a, c) for a in range(PASSES)])
+                other = ring.tile([P, CHUNK], F32, name="other", bufs=4)
+                nc.scalar.copy(other[:], acc[:, 1, 0:CHUNK])
+                nc.vector.tensor_tensor(h1[t][:, cols], acc[:, 0, 0:CHUNK], other[:], MAX)
+
+        def make_z1(c):
+            cols = slice(c * CHUNK, (c + 1) * CHUNK)
+            rows = ring.tile([P, PACK, CHUNK], BF16, name="z1_rows")
+            for t in range(PACK):
+                squashed = ring.tile([P, CHUNK], F32, name="squashed")
+                nc.scalar.activation(squashed[:], h1[t][:, cols], TANH)
+                nc.scalar.activation(rows[:, t, :], squashed[:], COPY, scale=gains[:, t : t + 1])
+            return quantize("z1_%d" % c, interleave(nc.scalar.copy, "z_bf16", rows[:], CHUNK), CHUNK)
+
+        def place(b, passes, width, offsets, factors):
+            acc = psum.tile([P, BANK], F32, name="acc_y", bufs=4)
+            passes_into(acc[:, 0:width], passes)
+            y = ring.tile([P, BANK], F32, name="y", bufs=6)
+            nc.scalar.copy(y[:, 0:width], acc[:, 0:width])
+            nc.vector.tensor_tensor(pages[b][:].indirect(offsets), y[:, 0:width], factors, MULT)
+
+        def second_stage(c, z1):
+            cols = slice(c * CHUNK, (c + 1) * CHUNK)
+            for b in range(ROW_BLOCKS):
+                m = slice(b * P, (b + 1) * P)
+                passes = [(w5_codes[:, a, m].bitcast(FP8X4), w5_planes[:, a * N + b * P : a * N + (b + 1) * P])
+                          + v_operand(a, c) for a in range(PASSES)]
+                passes.append((w4_q[0][:, m].bitcast(FP8X4), w4_q[1][:, m], z1[0][:].bitcast(FP8X4), z1[1][:]))
+                place(b, passes, CHUNK, idx3[:, c * first_cols : (c + 1) * first_cols], wg1_sb[:, cols])
+
+        first_stage(0)
+        w4_q = quantize("w4", interleave(nc.vector.tensor_copy, "weight_bf16", w4_raw[:], N), N)
+        for c in range(CHUNKS - 2):
+            z1 = make_z1(c)
+            first_stage(c + 1)
+            second_stage(c, z1)
+
+        v2_words = gather("v2_words", tab2_sb[:], idx2[:], U32)
+        v2_plane = gather("v2_plane", tab2_plane[:], idx2[:], U8)
+        w3_q = quantize("w3", round_first_weight(nc.scalar.copy, w3_raw), H)
+        h2 = []
+        for t in range(PACK):
+            m = slice(t * P, (t + 1) * P)
+            acc = psum.tile([P, BANK], F32, name="acc_y", bufs=4)
+            passes_into(acc[:], [(w3_q[0][:, m].bitcast(FP8X4), w3_q[1][:, m], v2_words[:].bitcast(FP8X4), v2_plane[:])])
+            rows = held("h2_%d" % t, [P, B], F32)
+            nc.scalar.copy(rows[:], acc[:])
+            h2.append(rows)
+
+        z1 = make_z1(CHUNKS - 2)
+        first_stage(CHUNKS - 1)
+        z2_rows = held("z2_rows", [P, PACK, B], F32)
+        for t in range(PACK):
+            nc.vector.tensor_tensor(z2_rows[:, t, :], h1[t][:].indirect(hero[:]), h2[t][:], MULT)
+        second_stage(CHUNKS - 2, z1)
+
+        z1 = make_z1(CHUNKS - 1)
+        w6_q = quantize("w6", interleave(nc.scalar.copy, "weight_bf16", w6_raw[:], N), N)
+        z2 = quantize("z2", interleave(nc.scalar.copy, "z_bf16", z2_rows[:], B), B)
+        second_stage(CHUNKS - 1, z1)
+        for b in range(ROW_BLOCKS):
+            m = slice(b * P, (b + 1) * P)
+            place(b, [(w6_q[0][:, m].bitcast(FP8X4), w6_q[1][:, m], z2[0][:].bitcast(FP8X4), z2[1][:])],
+                  B, idx4[:], wg2_sb[:])
+            nc.sync.dma_start(out[b * P : (b + 1) * P, :], pages[b][:])

@@ -58,6 +58,11 @@ def tile_list_showroom_slot_features_kernel(
                 )
             return tile
 
+        def load_page(b):
+            page = held("page%d" % b, [P, T2], F32)
+            nc.sync.dma_start(page[:], page1[b * P : (b + 1) * P, :])
+            return page
+
         def load_table_pass(name, words):
             tile = held(name, [P, T], U32)
             nc.sync.dma_start(tile[:].bitcast(I32), words.rearrange("p t i -> p (t i)").bitcast(I32))
@@ -80,22 +85,28 @@ def tile_list_showroom_slot_features_kernel(
             nc.vector.tensor_copy(tile[:], window.indirect(offsets))
             return tile
 
-        def quantize(name, grouped, width):
-            codes = held(name + "_codes", [P, width], U32)
+        def quantize(name, grouped, width, slot=None):
+            codes = held(slot or name + "_codes", [P, width], U32)
             scales = held(name + "_scales", [P, width], U8)
             nc.vector.quantize_mx(out=codes[:].bitcast(FP8X4), scales=scales[:], in_=grouped[:, 0 : PACK * width])
             return codes, scales
 
-        def round_first_weight(move, raw):
-            grouped = ring.tile([P, PACK * H], BF16, name="weight_bf16", align_bytes=64)
+        def round_first_weight(move, raw, slot=None):
+            if slot:
+                grouped = held(slot, [P, PACK * H], BF16)
+            else:
+                grouped = ring.tile([P, PACK * H], BF16, name="weight_bf16", align_bytes=64)
             move(
                 grouped[:].rearrange("p (t u e j) -> p t u j e", t=PACK, e=4, j=PACK),
                 raw[:].rearrange("p j (u t e) -> p t u j e", t=PACK, e=4),
             )
             return grouped
 
-        def interleave(move, tag, rows, width):
-            grouped = ring.tile([P, PACK * BANK], BF16, name=tag, align_bytes=64)
+        def interleave(move, tag, rows, width, slot=None):
+            if slot:
+                grouped = held(slot, [P, PACK * width], BF16)
+            else:
+                grouped = ring.tile([P, PACK * BANK], BF16, name=tag, align_bytes=64)
             move(
                 grouped[:, 0 : PACK * width].rearrange("p (c i t) -> p c t i", i=4, t=PACK),
                 rows.rearrange("p t (c i) -> p c t i", i=4),
@@ -107,45 +118,47 @@ def tile_list_showroom_slot_features_kernel(
                 nc.tensor.matmul_mx(out=acc, lhsT=w_codes, lhsT_scale=w_scales, rhs=x_codes, rhs_scale=x_scales,
                                     start=(i == 0), stop=(i == len(passes) - 1))
 
-        idx = load_list("idx", offs)
-        tab_planes = load_planes(nc.scalar, nc.vector, "tab_planes", tab_scales)
         tab_sb = [None] * PASSES
+        w1_raw = [None] * PASSES
+        pages = [None] * ROW_BLOCKS
+        idx = load_list("idx", offs)
+        idx3 = load_list("idx3", offs3)
+        idx2 = load_list("idx2", offs2)
+        tab_planes = load_planes(nc.sync, nc.vector, "tab_planes", tab_scales)
         tab_sb[0] = load_table_pass("tab0", tab_words[0])
-        w2_planes_raw = load_planes(nc.sync, nc.gpsimd, "w2_planes_raw", w2_scales)
+        w1_raw[0] = load_first_weight("w1_raw0", w1[0:K_PASS, :])
         w2_raw = held("w2_raw", [P, PASSES, H // 2], I32)
         nc.sync.dma_start(w2_raw[:], w2_words.bitcast(I32).rearrange("a p c -> p a c"))
-        w1_raw = [load_first_weight("w1_raw%d" % a, w1[a * K_PASS : (a + 1) * K_PASS, :]) for a in range(PASSES)]
+        w1_raw[1] = load_first_weight("w1_raw1", w1[K_PASS:K, :])
+        w2_planes_raw = load_planes(nc.sync, nc.gpsimd, "w2_planes_raw", w2_scales)
+        w4_raw = load_second_weight("w4_raw", w4)
         tab_sb[1] = load_table_pass("tab1", tab_words[1])
         gains = held("gains", [P, PACK], F32)
         with nc.allow_non_contiguous_dma(reason="one gain to a partition and slot"):
             for e in range(4):
                 nc.sync.dma_start(gains[e:P:4, :], gain.rearrange("(u t e) -> e u t", t=PACK, e=4)[e])
-        w4_raw = load_second_weight("w4_raw", w4)
         w5_codes = held("w5_codes", [P, PASSES, N], U32)
         nc.sync.dma_start(w5_codes[:].bitcast(I32), w5_words.rearrange("a p c i -> p a (c i)").bitcast(I32))
         w5_planes = load_planes(nc.sync, nc.gpsimd, "w5_planes", w5_scales)
-        idx3 = load_list("idx3", offs3)
-        wg1_sb = held("wg1_sb", [P, S], F32)
-        nc.sync.dma_start(wg1_sb[:], wg1)
-        pages = []
-        for b in range(ROW_BLOCKS):
-            page = held("page%d" % b, [P, T2], F32)
-            nc.sync.dma_start(page[:], page1[b * P : (b + 1) * P, :])
-            pages.append(page)
-        idx2 = load_list("idx2", offs2)
-        tab2_sb = load_table_pass("tab2", tab2_words[0])
         tab2_plane = load_planes(nc.sync, nc.gpsimd, "tab2_plane", tab2_scales)
+        tab2_sb = load_table_pass("tab2", tab2_words[0])
+        pages[0] = load_page(0)
+        wg1_first = held("wg1_first", [P, CHUNK], F32)
+        nc.sync.dma_start(wg1_first[:], wg1[:, 0:CHUNK])
+        pages[1] = load_page(1)
         w3_raw = load_first_weight("w3_raw", w3)
+        pages[2] = load_page(2)
+        wg1_rest = held("wg1_rest", [P, S - CHUNK], F32)
+        nc.sync.dma_start(wg1_rest[:], wg1[:, CHUNK:S])
         hero = load_list("hero", pos1)
         w6_raw = load_second_weight("w6_raw", w6)
         idx4 = load_list("idx4", offs4)
         wg2_sb = held("wg2_sb", [P, B], F32)
         nc.sync.dma_start(wg2_sb[:], wg2)
 
-        v_words0 = gather("v_words0", tab_sb[0][:], idx[:], U32)
         first_cols = CHUNK // 16
-        planes_first = [gather("v_plane_first%d" % a, tab_planes[:, a * T : (a + 1) * T], idx[:, 0:first_cols], U8)
-                        for a in range(PASSES)]
+        v_planes = [gather("v_plane%d" % a, tab_planes[:, a * T : (a + 1) * T], idx[:], U8) for a in range(PASSES)]
+        v_words0 = gather("v_words0", tab_sb[0][:], idx[:], U32)
         w2_codes = held("w2_codes", [P, PASSES * 2 * H], U8)
         nc.vector.tensor_copy(
             w2_codes[:].bitcast(I32).rearrange("p (a t u h) -> p a t u h", a=PASSES, t=PACK, h=2),
@@ -159,8 +172,6 @@ def tile_list_showroom_slot_features_kernel(
         w1_q = [quantize("w1_%d" % a, round_first_weight(nc.scalar.copy, w1_raw[a]), H) for a in range(PASSES)]
         v_words1_first = gather("v_words1_first", tab_sb[1][:], idx[:, 0:first_cols], U32)
         v_words1_rest = gather("v_words1_rest", tab_sb[1][:], idx[:, first_cols : S // 16], U32)
-        planes_rest = [gather("v_plane_rest%d" % a, tab_planes[:, a * T : (a + 1) * T], idx[:, first_cols : S // 16], U8)
-                       for a in range(PASSES)]
 
         def v_operand(a, c):
             cols = slice(c * CHUNK, (c + 1) * CHUNK)
@@ -170,80 +181,101 @@ def tile_list_showroom_slot_features_kernel(
                 words = v_words1_first[:]
             else:
                 words = v_words1_rest[:, (c - 1) * CHUNK : c * CHUNK]
-            plane = planes_first[a][:] if c == 0 else planes_rest[a][:, (c - 1) * CHUNK : c * CHUNK]
-            return words.bitcast(FP8X4), plane
+            return words.bitcast(FP8X4), v_planes[a][:, cols]
 
         h1 = [held("h1_%d" % t, [P, S], F32) for t in range(PACK)]
 
+        def first_stage_pass(acc, c, t, a):
+            x_codes, x_scales = v_operand(a, c)
+            m = slice(t * P, (t + 1) * P)
+            nc.tensor.matmul_mx(out=acc[:, 0, :], lhsT=w1_q[a][0][:, m].bitcast(FP8X4), lhsT_scale=w1_q[a][1][:, m],
+                                rhs=x_codes, rhs_scale=x_scales, start=(a == 0), stop=False)
+            nc.tensor.matmul_mx(out=acc[:, 1, :],
+                                lhsT=w2_codes[:, 2 * (a * H + t * P) : 2 * (a * H + (t + 1) * P)].bitcast(FP4X4),
+                                lhsT_scale=w2_planes[:, a * H + t * P : a * H + (t + 1) * P],
+                                rhs=x_codes, rhs_scale=x_scales, start=False, stop=(a == PASSES - 1))
+
         def first_stage(c):
             cols = slice(c * CHUNK, (c + 1) * CHUNK)
+            accs = [psum.tile([P, 2, CHUNK], F32, name="acc_h1", bufs=4) for t in range(PACK)]
+            others = held("zi_1" if c == 2 else "turn_a%d" % (c % 2), [P, PACK, CHUNK], F32)
+            early = PASSES - 1 if c == 0 else 0
+            for a in range(early):
+                for t in range(PACK):
+                    first_stage_pass(accs[t], c, t, a)
             for t in range(PACK):
-                m = slice(t * P, (t + 1) * P)
-                acc = psum.tile([P, 2, CHUNK], F32, name="acc_h1", bufs=4)
-                passes_into(acc[:, 1, 0:CHUNK], [
-                    (w2_codes[:, 2 * (a * H + t * P) : 2 * (a * H + (t + 1) * P)].bitcast(FP4X4),
-                     w2_planes[:, a * H + t * P : a * H + (t + 1) * P]) + v_operand(a, c) for a in range(PASSES)])
-                passes_into(acc[:, 0, 0:CHUNK], [
-                    (w1_q[a][0][:, m].bitcast(FP8X4), w1_q[a][1][:, m]) + v_operand(a, c) for a in range(PASSES)])
-                other = ring.tile([P, CHUNK], F32, name="other", bufs=4)
-                nc.scalar.copy(other[:], acc[:, 1, 0:CHUNK])
-                nc.vector.tensor_tensor(h1[t][:, cols], acc[:, 0, 0:CHUNK], other[:], MAX)
+                for a in range(early, PASSES):
+                    first_stage_pass(accs[t], c, t, a)
+                nc.scalar.copy(others[:, t, :], accs[t][:, 1, :])
+                nc.vector.tensor_tensor(h1[t][:, cols], accs[t][:, 0, :], others[:, t, :], MAX)
 
         def make_z1(c):
             cols = slice(c * CHUNK, (c + 1) * CHUNK)
-            rows = ring.tile([P, PACK, CHUNK], BF16, name="z1_rows")
+            rows = held("z1_rows%d" % (c % 2), [P, PACK, CHUNK], BF16)
             for t in range(PACK):
                 squashed = ring.tile([P, CHUNK], F32, name="squashed")
                 nc.scalar.activation(squashed[:], h1[t][:, cols], TANH)
                 nc.scalar.activation(rows[:, t, :], squashed[:], COPY, scale=gains[:, t : t + 1])
-            return quantize("z1_%d" % c, interleave(nc.scalar.copy, "z_bf16", rows[:], CHUNK), CHUNK)
+            return quantize("z1_%d" % c, interleave(nc.vector.tensor_copy if c == 0 else nc.scalar.copy, "z_bf16", rows[:], CHUNK,
+                                                 "zi_%d" % c), CHUNK,
+                            "w3_bf16" if c == 1 else "z1_codes%d" % c)
 
-        def place(b, passes, width, offsets, factors):
+        def place(b, passes, width, offsets, factors, slot=None):
             acc = psum.tile([P, BANK], F32, name="acc_y", bufs=4)
             passes_into(acc[:, 0:width], passes)
-            y = ring.tile([P, BANK], F32, name="y", bufs=6)
+            y = held(slot, [P, width], F32) if slot else ring.tile([P, BANK], F32, name="y", bufs=3)
             nc.scalar.copy(y[:, 0:width], acc[:, 0:width])
             nc.vector.tensor_tensor(pages[b][:].indirect(offsets), y[:, 0:width], factors, MULT)
 
-        def second_stage(c, z1):
+        def y_slot(c, b):
+            if b == 1:
+                return "turn_a%d" % (c % 2)
+            if c == CHUNKS - 1:
+                return "h2_2" if b == 0 else "z2_rows"
+            if b == 2:
+                return "w3_codes" if c == 0 else "z1_codes%d" % (c + 1)
+            return None
+
+        def second_stage(c, z1, blocks):
             cols = slice(c * CHUNK, (c + 1) * CHUNK)
-            for b in range(ROW_BLOCKS):
+            for b in blocks:
                 m = slice(b * P, (b + 1) * P)
                 passes = [(w5_codes[:, a, m].bitcast(FP8X4), w5_planes[:, a * N + b * P : a * N + (b + 1) * P])
                           + v_operand(a, c) for a in range(PASSES)]
                 passes.append((w4_q[0][:, m].bitcast(FP8X4), w4_q[1][:, m], z1[0][:].bitcast(FP8X4), z1[1][:]))
-                place(b, passes, CHUNK, idx3[:, c * first_cols : (c + 1) * first_cols], wg1_sb[:, cols])
+                place(b, passes, CHUNK, idx3[:, c * first_cols : (c + 1) * first_cols], wg1_first[:] if c == 0 else wg1_rest[:, (c - 1) * CHUNK : c * CHUNK], y_slot(c, b))
 
+        z1 = [None] * CHUNKS
+        w4_q = quantize("w4", interleave(nc.scalar.copy, "weight_bf16", w4_raw[:], N), N)
         first_stage(0)
-        w4_q = quantize("w4", interleave(nc.vector.tensor_copy, "weight_bf16", w4_raw[:], N), N)
-        for c in range(CHUNKS - 2):
-            z1 = make_z1(c)
-            first_stage(c + 1)
-            second_stage(c, z1)
-
         v2_words = gather("v2_words", tab2_sb[:], idx2[:], U32)
         v2_plane = gather("v2_plane", tab2_plane[:], idx2[:], U8)
-        w3_q = quantize("w3", round_first_weight(nc.scalar.copy, w3_raw), H)
-        h2 = []
-        for t in range(PACK):
+        z1[0] = make_z1(0)
+        first_stage(1)
+        second_stage(0, z1[0], range(ROW_BLOCKS))
+        w3_q = quantize("w3", round_first_weight(nc.scalar.copy, w3_raw, "w3_bf16"), H)
+        z1[1] = make_z1(1)
+        first_stage(2)
+        second_stage(1, z1[1], range(ROW_BLOCKS))
+        z1[2] = make_z1(2)
+        first_stage(3)
+        second_stage(2, z1[2], range(ROW_BLOCKS))
+        def make_h2(t, slot):
             m = slice(t * P, (t + 1) * P)
             acc = psum.tile([P, BANK], F32, name="acc_y", bufs=4)
             passes_into(acc[:], [(w3_q[0][:, m].bitcast(FP8X4), w3_q[1][:, m], v2_words[:].bitcast(FP8X4), v2_plane[:])])
-            rows = held("h2_%d" % t, [P, B], F32)
+            rows = held(slot, [P, B], F32)
             nc.scalar.copy(rows[:], acc[:])
-            h2.append(rows)
-
-        z1 = make_z1(CHUNKS - 2)
-        first_stage(CHUNKS - 1)
+            return rows
+        h2 = [make_h2(t, "h2_%d" % t) for t in range(PACK - 1)]
+        z1[3] = make_z1(3)
+        h2.append(make_h2(PACK - 1, "z1_rows1"))
         z2_rows = held("z2_rows", [P, PACK, B], F32)
         for t in range(PACK):
             nc.vector.tensor_tensor(z2_rows[:, t, :], h1[t][:].indirect(hero[:]), h2[t][:], MULT)
-        second_stage(CHUNKS - 2, z1)
-
-        z1 = make_z1(CHUNKS - 1)
         w6_q = quantize("w6", interleave(nc.scalar.copy, "weight_bf16", w6_raw[:], N), N)
-        z2 = quantize("z2", interleave(nc.scalar.copy, "z_bf16", z2_rows[:], B), B)
-        second_stage(CHUNKS - 1, z1)
+        z2 = quantize("z2", interleave(nc.scalar.copy, "z_bf16", z2_rows[:], B, "zi_3"), B)
+        second_stage(3, z1[3], range(ROW_BLOCKS))
         for b in range(ROW_BLOCKS):
             m = slice(b * P, (b + 1) * P)
             place(b, [(w6_q[0][:, m].bitcast(FP8X4), w6_q[1][:, m], z2[0][:].bitcast(FP8X4), z2[1][:])],

@@ -97,8 +97,8 @@ def tile_list_showroom_slot_features_kernel(
             else:
                 grouped = ring.tile([P, PACK * H], BF16, name="weight_bf16", align_bytes=64)
             move(
-                grouped[:].rearrange("p (t u e j) -> p t u j e", t=PACK, e=4, j=PACK),
-                raw[:].rearrange("p j (u t e) -> p t u j e", t=PACK, e=4),
+                grouped[:].rearrange("p (t u e j) -> p t u e j", t=PACK, e=4, j=PACK),
+                raw[:].rearrange("p j (u t e) -> p t u e j", t=PACK, e=4),
             )
             return grouped
 
@@ -108,8 +108,8 @@ def tile_list_showroom_slot_features_kernel(
             else:
                 grouped = ring.tile([P, PACK * BANK], BF16, name=tag, align_bytes=64)
             move(
-                grouped[:, 0 : PACK * width].rearrange("p (c i t) -> p c t i", i=4, t=PACK),
-                rows.rearrange("p t (c i) -> p c t i", i=4),
+                grouped[:, 0 : PACK * width].rearrange("p (c t) -> p c t", t=PACK),
+                rows.rearrange("p t c -> p c t"),
             )
             return grouped
 
@@ -131,23 +131,23 @@ def tile_list_showroom_slot_features_kernel(
         nc.sync.dma_start(w2_raw[:], w2_words.bitcast(I32).rearrange("a p c -> p a c"))
         w1_raw[1] = load_first_weight("w1_raw1", w1[K_PASS:K, :])
         w2_planes_raw = load_planes(nc.sync, nc.gpsimd, "w2_planes_raw", w2_scales)
-        w4_raw = load_second_weight("w4_raw", w4)
         tab_sb[1] = load_table_pass("tab1", tab_words[1])
         gains = held("gains", [P, PACK], F32)
         with nc.allow_non_contiguous_dma(reason="one gain to a partition and slot"):
             for e in range(4):
                 nc.sync.dma_start(gains[e:P:4, :], gain.rearrange("(u t e) -> e u t", t=PACK, e=4)[e])
+        w4_raw = load_second_weight("w4_raw", w4)
         w5_codes = held("w5_codes", [P, PASSES, N], U32)
         nc.sync.dma_start(w5_codes[:].bitcast(I32), w5_words.rearrange("a p c i -> p a (c i)").bitcast(I32))
         w5_planes = load_planes(nc.sync, nc.gpsimd, "w5_planes", w5_scales)
-        tab2_plane = load_planes(nc.sync, nc.gpsimd, "tab2_plane", tab2_scales)
-        tab2_sb = load_table_pass("tab2", tab2_words[0])
         pages[0] = load_page(0)
         wg1_first = held("wg1_first", [P, CHUNK], F32)
         nc.sync.dma_start(wg1_first[:], wg1[:, 0:CHUNK])
         pages[1] = load_page(1)
         w3_raw = load_first_weight("w3_raw", w3)
         pages[2] = load_page(2)
+        tab2_plane = load_planes(nc.sync, nc.gpsimd, "tab2_plane", tab2_scales)
+        tab2_sb = load_table_pass("tab2", tab2_words[0])
         wg1_rest = held("wg1_rest", [P, S - CHUNK], F32)
         nc.sync.dma_start(wg1_rest[:], wg1[:, CHUNK:S])
         hero = load_list("hero", pos1)
@@ -185,29 +185,36 @@ def tile_list_showroom_slot_features_kernel(
 
         h1 = [held("h1_%d" % t, [P, S], F32) for t in range(PACK)]
 
-        def first_stage_pass(acc, c, t, a):
+        def first_stage_passes(accs, c, pair, a):
             x_codes, x_scales = v_operand(a, c)
-            m = slice(t * P, (t + 1) * P)
-            nc.tensor.matmul_mx(out=acc[:, 0, :], lhsT=w1_q[a][0][:, m].bitcast(FP8X4), lhsT_scale=w1_q[a][1][:, m],
-                                rhs=x_codes, rhs_scale=x_scales, start=(a == 0), stop=False)
-            nc.tensor.matmul_mx(out=acc[:, 1, :],
-                                lhsT=w2_codes[:, 2 * (a * H + t * P) : 2 * (a * H + (t + 1) * P)].bitcast(FP4X4),
-                                lhsT_scale=w2_planes[:, a * H + t * P : a * H + (t + 1) * P],
-                                rhs=x_codes, rhs_scale=x_scales, start=False, stop=(a == PASSES - 1))
+            for i in range(2):
+                t = 2 * pair + i
+                nc.tensor.matmul_mx(out=accs[1][:, i, :],
+                                    lhsT=w2_codes[:, 2 * (a * H + t * P) : 2 * (a * H + (t + 1) * P)].bitcast(FP4X4),
+                                    lhsT_scale=w2_planes[:, a * H + t * P : a * H + (t + 1) * P],
+                                    rhs=x_codes, rhs_scale=x_scales,
+                                    start=(a == 0 and i == 0), stop=(a == PASSES - 1 and i == 1))
+            for i in range(2):
+                m = slice((2 * pair + i) * P, (2 * pair + i + 1) * P)
+                nc.tensor.matmul_mx(out=accs[0][:, i, :], lhsT=w1_q[a][0][:, m].bitcast(FP8X4),
+                                    lhsT_scale=w1_q[a][1][:, m], rhs=x_codes, rhs_scale=x_scales,
+                                    start=(a == 0 and i == 0), stop=(a == PASSES - 1 and i == 1))
 
         def first_stage(c):
             cols = slice(c * CHUNK, (c + 1) * CHUNK)
-            accs = [psum.tile([P, 2, CHUNK], F32, name="acc_h1", bufs=4) for t in range(PACK)]
+            accs = [[psum.tile([P, 2, CHUNK], F32, name="acc_h1", bufs=4) for w in range(2)] for pair in range(2)]
             others = held("zi_1" if c == 2 else "turn_a%d" % (c % 2), [P, PACK, CHUNK], F32)
             early = PASSES - 1 if c == 0 else 0
             for a in range(early):
-                for t in range(PACK):
-                    first_stage_pass(accs[t], c, t, a)
-            for t in range(PACK):
+                for pair in range(2):
+                    first_stage_passes(accs[pair], c, pair, a)
+            for pair in range(2):
                 for a in range(early, PASSES):
-                    first_stage_pass(accs[t], c, t, a)
-                nc.scalar.copy(others[:, t, :], accs[t][:, 1, :])
-                nc.vector.tensor_tensor(h1[t][:, cols], accs[t][:, 0, :], others[:, t, :], MAX)
+                    first_stage_passes(accs[pair], c, pair, a)
+                nc.scalar.copy(others[:, 2 * pair : 2 * pair + 2, :], accs[pair][1][:])
+                for i in range(2):
+                    t = 2 * pair + i
+                    nc.vector.tensor_tensor(h1[t][:, cols], accs[pair][0][:, i, :], others[:, t, :], MAX)
 
         def make_z1(c):
             cols = slice(c * CHUNK, (c + 1) * CHUNK)
@@ -246,16 +253,16 @@ def tile_list_showroom_slot_features_kernel(
                 place(b, passes, CHUNK, idx3[:, c * first_cols : (c + 1) * first_cols], wg1_first[:] if c == 0 else wg1_rest[:, (c - 1) * CHUNK : c * CHUNK], y_slot(c, b))
 
         z1 = [None] * CHUNKS
-        w4_q = quantize("w4", interleave(nc.scalar.copy, "weight_bf16", w4_raw[:], N), N)
         first_stage(0)
-        v2_words = gather("v2_words", tab2_sb[:], idx2[:], U32)
-        v2_plane = gather("v2_plane", tab2_plane[:], idx2[:], U8)
+        w4_q = quantize("w4", interleave(nc.vector.tensor_copy, "weight_bf16", w4_raw[:], N), N)
         z1[0] = make_z1(0)
         first_stage(1)
         second_stage(0, z1[0], range(ROW_BLOCKS))
         w3_q = quantize("w3", round_first_weight(nc.scalar.copy, w3_raw, "w3_bf16"), H)
         z1[1] = make_z1(1)
         first_stage(2)
+        v2_words = gather("v2_words", tab2_sb[:], idx2[:], U32)
+        v2_plane = gather("v2_plane", tab2_plane[:], idx2[:], U8)
         second_stage(1, z1[1], range(ROW_BLOCKS))
         z1[2] = make_z1(2)
         first_stage(3)

from contextlib import ExitStack

import concourse.mybir as mybir

K, K2, H, N, T, S, B, T2 = 1024, 512, 512, 384, 2048, 1024, 512, 2048
FLOPS = 2 * (2 * K * H * S + K2 * H * B + H * N * S + K * N * S + H * N * B)

F32 = mybir.dt.float32
BF16 = mybir.dt.bfloat16
I32 = mybir.dt.int32
U32 = mybir.dt.uint32
U16 = mybir.dt.uint16
U8 = mybir.dt.uint8
FP8X4 = mybir.dt.float8_e4m3fn_x4
FP4X4 = mybir.dt.float4_e2m1fn_x4
MULT = mybir.AluOpType.mult
MAX = mybir.AluOpType.max
COPY = mybir.ActivationFunctionType.Copy
TANH = mybir.ActivationFunctionType.Tanh

P = 128
PACK = 4
K_PASS = P * PACK
PASSES = K // K_PASS
QUADS = 4
ROW_BLOCKS = N // P
CHUNK = 256
CHUNKS = S // CHUNK
BANK = 512


def tile_list_showroom_slot_features_kernel(
    tc, tab_words, tab_scales, tab2_words, tab2_scales, offs, offs2, pos1, offs3, offs4, w1, w2_words, w2_scales,
    w3, gain, w4, w5_words, w5_scales, w6, page1, wg1, wg2, out,
):
    nc = tc.nc
    with ExitStack() as ctx:
        keep = ctx.enter_context(tc.tile_pool(name="keep", bufs=1))
        ring = ctx.enter_context(tc.tile_pool(name="ring", bufs=2))
        psum = ctx.enter_context(tc.psum_pool(name="psum", bufs=2))

        def held(name, shape, dtype):
            return keep.tile(shape, dtype, name=name, align_bytes=64)

        def load_list(name, src):
            tile = keep.tile([P, src.shape[1]], U16, name=name)
            nc.sync.dma_start(tile[:], src)
            return tile

        def load_planes(queue, clear, name, src):
            passes, width = src.shape[0], src.shape[2]
            tile = held(name, [P, passes * width], U8)
            clear.memset(tile[:].bitcast(I32), 0)
            for q in range(QUADS):
                queue.dma_start(
                    tile[32 * q : 32 * q + 4, :].bitcast(I32).rearrange("r (a c) -> r a c", a=passes),
                    src[:, 4 * q : 4 * q + 4, :].bitcast(I32).rearrange("a r c -> r a c"),
                )
            return tile

        def load_page(b):
            page = held("page%d" % b, [P, T2], F32)
            nc.sync.dma_start(page[:], page1[b * P : (b + 1) * P, :])
            return page

        def load_table_pass(name, words):
            tile = held(name, [P, T], U32)
            nc.sync.dma_start(tile[:].bitcast(I32), words.rearrange("p t i -> p (t i)").bitcast(I32))
            return tile

        def load_first_weight(name, rows):
            tile = held(name, [P, PACK, H], F32)
            nc.sync.dma_start(tile[:], rows.rearrange("(p j) c -> p j c", j=PACK))
            return tile

        def load_second_weight(name, w):
            tile = held(name, [P, PACK, N], F32)
            rows = w.rearrange("(u t e) n -> t u e n", t=PACK, e=4)
            for t in range(PACK):
                nc.sync.dma_start(tile[:, t, :], rows[t])
            return tile

        def gather(name, window, offsets, dtype):
            tile = held(name, [P, 16 * offsets.shape[1]], dtype)
            nc.vector.tensor_copy(tile[:], window.indirect(offsets))
            return tile

        def quantize(name, grouped, width, slot=None):
            codes = held(slot or name + "_codes", [P, width], U32)
            scales = held(name + "_scales", [P, width], U8)
            nc.vector.quantize_mx(out=codes[:].bitcast(FP8X4), scales=scales[:], in_=grouped[:, 0 : PACK * width])
            return codes, scales

        def round_first_weight(move, raw, slot=None):
            if slot:
                grouped = held(slot, [P, PACK * H], BF16)
            else:
                grouped = ring.tile([P, PACK * H], BF16, name="weight_bf16", align_bytes=64)
            move(
                grouped[:].rearrange("p (t u e j) -> p t u e j", t=PACK, e=4, j=PACK),
                raw[:].rearrange("p j (u t e) -> p t u e j", t=PACK, e=4),
            )
            return grouped

        def interleave(move, tag, rows, width, slot=None):
            if slot:
                grouped = held(slot, [P, PACK * width], BF16)
            else:
                grouped = ring.tile([P, PACK * BANK], BF16, name=tag, align_bytes=64)
            move(
                grouped[:, 0 : PACK * width].rearrange("p (c t) -> p c t", t=PACK),
                rows.rearrange("p t c -> p c t"),
            )
            return grouped

        def passes_into(acc, passes):
            for i, (w_codes, w_scales, x_codes, x_scales) in enumerate(passes):
                nc.tensor.matmul_mx(out=acc, lhsT=w_codes, lhsT_scale=w_scales, rhs=x_codes, rhs_scale=x_scales,
                                    start=(i == 0), stop=(i == len(passes) - 1))

        tab_sb = [None] * PASSES
        w1_raw = [None] * PASSES
        pages = [None] * ROW_BLOCKS
        idx = load_list("idx", offs)
        idx3 = load_list("idx3", offs3)
        idx2 = load_list("idx2", offs2)
        tab_planes = load_planes(nc.sync, nc.vector, "tab_planes", tab_scales)
        tab_sb[0] = load_table_pass("tab0", tab_words[0])
        w1_raw[0] = load_first_weight("w1_raw0", w1[0:K_PASS, :])
        w2_raw = held("w2_raw", [P, PASSES, H // 2], I32)
        nc.sync.dma_start(w2_raw[:], w2_words.bitcast(I32).rearrange("a p c -> p a c"))
        w1_raw[1] = load_first_weight("w1_raw1", w1[K_PASS:K, :])
        w2_planes_raw = load_planes(nc.sync, nc.gpsimd, "w2_planes_raw", w2_scales)
        tab_sb[1] = load_table_pass("tab1", tab_words[1])
        gains = held("gains", [P, PACK], F32)
        with nc.allow_non_contiguous_dma(reason="one gain to a partition and slot"):
            for e in range(4):
                nc.sync.dma_start(gains[e:P:4, :], gain.rearrange("(u t e) -> e u t", t=PACK, e=4)[e])
        w4_raw = load_second_weight("w4_raw", w4)
        w5_codes = held("w5_codes", [P, PASSES, N], U32)
        nc.sync.dma_start(w5_codes[:].bitcast(I32), w5_words.rearrange("a p c i -> p a (c i)").bitcast(I32))
        w5_planes = load_planes(nc.sync, nc.gpsimd, "w5_planes", w5_scales)
        pages[0] = load_page(0)
        wg1_first = held("wg1_first", [P, CHUNK], F32)
        nc.sync.dma_start(wg1_first[:], wg1[:, 0:CHUNK])
        pages[1] = load_page(1)
        w3_raw = load_first_weight("w3_raw", w3)
        pages[2] = load_page(2)
        tab2_plane = load_planes(nc.sync, nc.gpsimd, "tab2_plane", tab2_scales)
        tab2_sb = load_table_pass("tab2", tab2_words[0])
        wg1_rest = held("wg1_rest", [P, S - CHUNK], F32)
        nc.sync.dma_start(wg1_rest[:], wg1[:, CHUNK:S])
        hero = load_list("hero", pos1)
        w6_raw = load_second_weight("w6_raw", w6)
        idx4 = load_list("idx4", offs4)
        wg2_sb = held("wg2_sb", [P, B], F32)
        nc.sync.dma_start(wg2_sb[:], wg2)

        first_cols = CHUNK // 16
        v_planes = [gather("v_plane%d" % a, tab_planes[:, a * T : (a + 1) * T], idx[:], U8) for a in range(PASSES)]
        v_words0 = gather("v_words0", tab_sb[0][:], idx[:], U32)
        w2_codes = held("w2_codes", [P, PASSES * 2 * H], U8)
        nc.vector.tensor_copy(
            w2_codes[:].bitcast(I32).rearrange("p (a t u h) -> p a t u h", a=PASSES, t=PACK, h=2),
            w2_raw[:].rearrange("p a (u t h) -> p a t u h", t=PACK, h=2),
        )
        w2_planes = held("w2_planes", [P, PASSES * H], U8)
        nc.vector.tensor_copy(
            w2_planes[:].bitcast(I32).rearrange("p (a t u) -> p a t u", a=PASSES, t=PACK),
            w2_planes_raw[:].bitcast(I32).rearrange("p (a u t) -> p a t u", a=PASSES, t=PACK),
        )
        w1_q = [quantize("w1_%d" % a, round_first_weight(nc.scalar.copy, w1_raw[a]), H) for a in range(PASSES)]
        v_words1_first = gather("v_words1_first", tab_sb[1][:], idx[:, 0:first_cols], U32)
        v_words1_rest = gather("v_words1_rest", tab_sb[1][:], idx[:, first_cols : S // 16], U32)

        def v_operand(a, c):
            cols = slice(c * CHUNK, (c + 1) * CHUNK)
            if a == 0:
                words = v_words0[:, cols]
            elif c == 0:
                words = v_words1_first[:]
            else:
                words = v_words1_rest[:, (c - 1) * CHUNK : c * CHUNK]
            return words.bitcast(FP8X4), v_planes[a][:, cols]

        h1 = [held("h1_%d" % t, [P, S], F32) for t in range(PACK)]

        def first_stage_passes(accs, c, pair, a):
            x_codes, x_scales = v_operand(a, c)
            for i in range(2):
                t = 2 * pair + i
                nc.tensor.matmul_mx(out=accs[1][:, i, :],
                                    lhsT=w2_codes[:, 2 * (a * H + t * P) : 2 * (a * H + (t + 1) * P)].bitcast(FP4X4),
                                    lhsT_scale=w2_planes[:, a * H + t * P : a * H + (t + 1) * P],
                                    rhs=x_codes, rhs_scale=x_scales,
                                    start=(a == 0 and i == 0), stop=(a == PASSES - 1 and i == 1))
            for i in range(2):
                m = slice((2 * pair + i) * P, (2 * pair + i + 1) * P)
                nc.tensor.matmul_mx(out=accs[0][:, i, :], lhsT=w1_q[a][0][:, m].bitcast(FP8X4),
                                    lhsT_scale=w1_q[a][1][:, m], rhs=x_codes, rhs_scale=x_scales,
                                    start=(a == 0 and i == 0), stop=(a == PASSES - 1 and i == 1))

        def first_stage(c):
            cols = slice(c * CHUNK, (c + 1) * CHUNK)
            accs = [[psum.tile([P, 2, CHUNK], F32, name="acc_h1", bufs=4) for w in range(2)] for pair in range(2)]
            others = held("zi_1" if c == 2 else "turn_a%d" % (c % 2), [P, PACK, CHUNK], F32)
            early = PASSES - 1 if c == 0 else 0
            for a in range(early):
                for pair in range(2):
                    first_stage_passes(accs[pair], c, pair, a)
            for pair in range(2):
                for a in range(early, PASSES):
                    first_stage_passes(accs[pair], c, pair, a)
                nc.scalar.copy(others[:, 2 * pair : 2 * pair + 2, :], accs[pair][1][:])
                for i in range(2):
                    t = 2 * pair + i
                    nc.vector.tensor_tensor(h1[t][:, cols], accs[pair][0][:, i, :], others[:, t, :], MAX)

        def make_z1(c):
            cols = slice(c * CHUNK, (c + 1) * CHUNK)
            rows = held("z1_rows%d" % (c % 2), [P, PACK, CHUNK], BF16)
            for t in range(PACK):
                squashed = ring.tile([P, CHUNK], F32, name="squashed")
                nc.scalar.activation(squashed[:], h1[t][:, cols], TANH)
                nc.scalar.activation(rows[:, t, :], squashed[:], COPY, scale=gains[:, t : t + 1])
            return quantize("z1_%d" % c, interleave(nc.vector.tensor_copy if c == 0 else nc.scalar.copy, "z_bf16", rows[:], CHUNK,
                                                 "zi_%d" % c), CHUNK,
                            "w3_bf16" if c == 1 else "z1_codes%d" % c)

        def place(b, passes, width, offsets, factors, slot=None):
            acc = psum.tile([P, BANK], F32, name="acc_y", bufs=4)
            passes_into(acc[:, 0:width], passes)
            y = held(slot, [P, width], F32) if slot else ring.tile([P, BANK], F32, name="y", bufs=3)
            nc.scalar.copy(y[:, 0:width], acc[:, 0:width])
            nc.vector.tensor_tensor(pages[b][:].indirect(offsets), y[:, 0:width], factors, MULT)

        def y_slot(c, b):
            if b == 1:
                return "turn_a%d" % (c % 2)
            if c == CHUNKS - 1:
                return "h2_2" if b == 0 else "z2_rows"
            if b == 2:
                return "w3_codes" if c == 0 else "z1_codes%d" % (c + 1)
            return None

        def second_stage(c, z1, blocks):
            cols = slice(c * CHUNK, (c + 1) * CHUNK)
            for b in blocks:
                m = slice(b * P, (b + 1) * P)
                passes = [(w5_codes[:, a, m].bitcast(FP8X4), w5_planes[:, a * N + b * P : a * N + (b + 1) * P])
                          + v_operand(a, c) for a in range(PASSES)]
                passes.append((w4_q[0][:, m].bitcast(FP8X4), w4_q[1][:, m], z1[0][:].bitcast(FP8X4), z1[1][:]))
                place(b, passes, CHUNK, idx3[:, c * first_cols : (c + 1) * first_cols], wg1_first[:] if c == 0 else wg1_rest[:, (c - 1) * CHUNK : c * CHUNK], y_slot(c, b))

        z1 = [None] * CHUNKS
        first_stage(0)
        w4_q = quantize("w4", interleave(nc.vector.tensor_copy, "weight_bf16", w4_raw[:], N), N)
        z1[0] = make_z1(0)
        first_stage(1)
        second_stage(0, z1[0], range(ROW_BLOCKS))
        w3_q = quantize("w3", round_first_weight(nc.scalar.copy, w3_raw, "w3_bf16"), H)
        z1[1] = make_z1(1)
        first_stage(2)
        v2_words = gather("v2_words", tab2_sb[:], idx2[:], U32)
        v2_plane = gather("v2_plane", tab2_plane[:], idx2[:], U8)
        second_stage(1, z1[1], range(ROW_BLOCKS))
        z1[2] = make_z1(2)
        first_stage(3)
        second_stage(2, z1[2], range(ROW_BLOCKS))
        def make_h2(t, slot):
            m = slice(t * P, (t + 1) * P)
            acc = psum.tile([P, BANK], F32, name="acc_y", bufs=4)
            passes_into(acc[:], [(w3_q[0][:, m].bitcast(FP8X4), w3_q[1][:, m], v2_words[:].bitcast(FP8X4), v2_plane[:])])
            rows = held(slot, [P, B], F32)
            nc.scalar.copy(rows[:], acc[:])
            return rows
        h2 = [make_h2(t, "h2_%d" % t) for t in range(PACK - 1)]
        z1[3] = make_z1(3)
        h2.append(make_h2(PACK - 1, "z1_rows1"))
        z2_rows = held("z2_rows", [P, PACK, B], F32)
        for t in range(PACK):
            nc.vector.tensor_tensor(z2_rows[:, t, :], h1[t][:].indirect(hero[:]), h2[t][:], MULT)
        w6_q = quantize("w6", interleave(nc.scalar.copy, "weight_bf16", w6_raw[:], N), N)
        z2 = quantize("z2", interleave(nc.scalar.copy, "z_bf16", z2_rows[:], B, "zi_3"), B)
        second_stage(3, z1[3], range(ROW_BLOCKS))
        for b in range(ROW_BLOCKS):
            m = slice(b * P, (b + 1) * P)
            place(b, [(w6_q[0][:, m].bitcast(FP8X4), w6_q[1][:, m], z2[0][:].bitcast(FP8X4), z2[1][:])],
                  B, idx4[:], wg2_sb[:])
            nc.sync.dma_start(out[b * P : (b + 1) * P, :], pages[b][:])
